import numpy as np, ml_dtypes
CORES = [1,5,17,21,33,37,49,53]
N = 8
BF = ml_dtypes.bfloat16
W, L, P, ST, IP = 4096, 256, 16, 4, 0.0625
def probes(s, w):
    u = np.sum(w[:, :, 0:1] * s, axis=1); v = 2 * (np.sum(w[:, :, 1:2] * s, axis=1) & (W // 2 - 1)) + 1
    return (u[:, None, :] + np.arange(P)[None, :, None] * v[:, None, :]) & (W - 1)
def margins(rng, share):
    k = (N, 8, 1, W)
    return np.where(rng.random(k) < share, 0.03 * rng.random(k), 0.1 + 0.4 * rng.random(k))
def sizes(rng):
    return rng.choice(np.array([0, 2, 6, 20]), (N, 8, 1, W))
def rules(rng, z, m):
    h = (N, 8, 16, W); m = m.astype(np.float32); z = np.minimum(z, 0.5).astype(np.float32)
    e = (np.minimum(np.floor((2 * m + 1) * rng.random(h, dtype=np.float32)), 2 * m) - m).astype(np.int32)
    a = np.maximum(0, -e); b = 255 - np.maximum(0, e)
    lo = a + np.floor(z * rng.random(h, dtype=np.float32) * (b - a)).astype(np.int32)
    hi = b - np.floor(z * rng.random(h, dtype=np.float32) * (b - a)).astype(np.int32)
    return lo, hi, e
def start(rng):
    s = rng.integers(0, 256, (N, 8, 16, L)); s = np.where(rng.random((N, 8, 1, L)) < 0.5, s, 64 + s // 2)
    return s, rng.integers(0, 2048, (N, 8, 16, 2)), rng.integers(0, 256, (N, 8, 16, ST)) >> rng.integers(0, 4, (N, 8, 16, ST))
def put(lo, hi, e, q, g, c, a, b, f):
    c, k = np.unique(c, return_index=True)
    lo[q, g][:, c] = a[:, k]; hi[q, g][:, c] = b[:, k]; e[q, g][:, c] = f[:, k]
def pack(lo, hi, e, s, w, d):
    t = lambda x: np.ascontiguousarray(x.reshape(N, 128, -1)).astype(np.float32).astype(BF)
    return {"lo": t(lo), "hi": t(hi), "ef": t(e), "s0": t(s), "wt": np.ascontiguousarray(w.reshape(N, 128, 2)).astype(np.int32), "dr": t(d)}
def setup_inputs(rng):
    share = rng.choice(np.array([1.5, 2.5, 4.0, 6.0]), (N, 8, 1, 1)) * IP
    return pack(*rules(rng, margins(rng, share), sizes(rng)), *start(rng))
def setup_inputs_alike(rng):
    z = margins(rng, 3 * IP); z[:, ::2] = 0.1
    lo, hi, e = rules(rng, z, sizes(rng)); s, w, d = start(rng)
    w[:, 0] = 0; w[:, 4] = 0; w[:, 2] = 0; w[:, 2, 0, 0] = 1; w[:, 6] = 0; w[:, 6, 15, 1] = W // 2 - 1; s[:, 6, 15] = 1
    k = rng.integers(0, 5, (N, 4, 1, L)); s[:, 1::2] = np.take_along_axis(s[:, 1::2, :, :5], k, 3)
    s[:, 5] = 255; s[:, 5, 15] = 255 - rng.integers(0, 4, (N, L)); s[:, 5, 15, :4] = 255 - np.arange(4)
    w[:, 5, :, 0] = 2047; w[:, 5, :, 1] = 0; w[:, 5, 0, 1] = 257
    x = np.full((8, 16, 4), 255); x[:, 15] = 255 - np.arange(4); b = x[5]
    for q in range(N):
        c = probes(x, w[q])[5]; a = rng.integers(0, 200, (16, 4 * P))
        put(lo, hi, e, q, 5, c.reshape(-1), a, a, 0 * a)
        a = b - rng.integers(0, 10, (16, 4)); a[15] = b[15]
        m = np.zeros((16, 4), np.int64); m[15] = np.arange(4) - rng.permutation(4)
        put(lo, hi, e, q, 5, c[P - 1], a, b, m)
    return pack(lo, hi, e, s, w, d)
def setup_inputs_chains(rng):
    lo, hi, e = rules(rng, margins(rng, 0.5 * IP), sizes(rng)); s, w, d = start(rng)
    s[:, ::2] = rng.choice(np.array([0, 1, 254, 255]), (N, 4, 16, L)); s[:, 2:4, :, 0] = 0
    for q in range(N):
        c = probes(s[q], w[q]); k = rng.choice(np.array([0, 1, 2, P // 2, P - 1]), (8, L)); k[2:4, 0] = 2
        for g in range(8): put(lo, hi, e, q, g, c[g, k[g], np.arange(L)], s[q, g], s[q, g], s[(q + 1) % N, g] - s[q, g])
    lo[:, 2:4, :, :2] = 1; hi[:, 2:4, :, :2] = 1; e[:, 2:4, :, :2] = 0
    d[:, 0] = 0; d[:, 1] = 255
    return pack(lo, hi, e, s, w, d)
def setup_inputs_full(rng):
    lo = rng.integers(0, 256, (N, 8, 16, W)); hi = lo.copy(); e = rng.integers(0, 256, (N, 8, 16, W)) - lo
    s, w, d = start(rng); s = rng.integers(100, 156, (N, 8, 16, L)); w = np.zeros((N, 8, 16, 2), np.int64); M = W // L; j = np.arange(L)
    for g in range(8):
        val = np.concatenate([rng.permutation(255)[:L - 1], np.array([255])]) if g % 2 == 0 else np.arange(L)
        for q in range(N):
            s[q, g, 0] = rng.permutation(val)
            if g % 2 == 0:
                s[q, g, 1] = 2; w[q, g, 0, 0] = 1; w[q, g, 1, 0] = 128 * (rng.integers(0, W // 256) if g < 6 else W // 256 - 1)
                k = np.full(L, rng.integers(0, 2))
            else:
                s[q, g, 1] = 1; w[q, g, 0, 0] = M; w[q, g, 1, 0] = rng.integers(0, M) if g < 7 else M - 1
                k = rng.integers(0, 2, L)
            w[q, g, 1, 1] = rng.integers(0, 2048)
            c = probes(s[q], w[q])[g]
            a = rng.integers(10, 65, (16, L)); b = rng.integers(191, 246, (16, L)); m = rng.integers(-9, 10, (16, L)); m[15] = rng.integers(1, 10, L)
            a[0] = s[q, g, 0]; b[0] = s[q, g, 0]; m[0] = rng.permutation(val) - s[q, g, 0]; a[1] = 0; b[1] = 255; m[1] = 0
            put(lo, hi, e, q, g, c[k, j], a, b, m)
    return pack(lo, hi, e, s, w, d)
def setup_inputs_ties(rng):
    lo, hi, e = rules(rng, margins(rng, 2.5 * IP), sizes(rng)); s, w, d = start(rng)
    for q in range(N):
        c = probes(s[q], w[q]); o = rng.permutation(8)
        for g in o[:2]:
            lo[q, g] = rng.integers(0, 256, (16, W)); hi[q, g] = lo[q, g]; e[q, g] = rng.integers(0, 256, (16, W)) - lo[q, g]
        for g in o[2:4]:
            lo[q, g] = 0; hi[q, g] = 255; e[q, g] = 0
        for g in o[4:]:
            x = s[q, g]; mode = rng.integers(0, 4, (1, L)); k = rng.integers(0, 3, L)
            one = (np.arange(16)[:, None] == rng.integers(0, 16, (1, L))) & (mode == 1)
            y = np.where(one, x + np.where(x < 128, 1, -1), x)
            a = np.where(mode == 3, np.floor(x * rng.random((16, L))).astype(np.int64), y)
            b = np.where(mode == 2, x + np.floor((255 - x) * rng.random((16, L))).astype(np.int64), y)
            put(lo, hi, e, q, g, c[g, k, np.arange(L)], a, b, np.minimum(np.maximum(rng.integers(-9, 10, (16, L)), -a), 255 - b))
    return pack(lo, hi, e, s, w, d)
def setup_inputs_spread(rng):
    k = (N, 8, 1, W)
    z = np.where(rng.random(k) < 6 * IP, np.exp2(-1 - 9 * rng.random(k)), 0.5)
    lo, hi, e = rules(rng, z, np.floor(np.exp2(8 * rng.random(k))) - 1); s, w, d = start(rng)
    s = np.floor(rng.random((N, 8, 16, L)) * np.exp2(rng.integers(0, 9, (N, 8, 1, L)))).astype(np.int64)
    s = np.where(rng.random((N, 8, 16, L)) < 0.3, 255 - s, s)
    w = np.floor(rng.random((N, 8, 16, 2)) * np.exp2(rng.integers(1, 12, (N, 8, 16, 2)))).astype(np.int64)
    d = np.floor(rng.random((N, 8, 16, ST)) * np.exp2(rng.integers(0, 9, (N, 8, 16, ST)))).astype(np.int64)
    return pack(lo, hi, e, s, w, d)
def check_inputs(d):
    bad = []; v = {k: np.asarray(d[k]).astype(np.float32) for k in ("lo", "hi", "ef", "s0", "dr")}
    for k in v:
        if not np.all(v[k] == np.floor(v[k])): bad.append("whole numbers in " + k)
    if not np.all((v["lo"] >= 0) & (v["lo"] <= v["hi"]) & (v["hi"] <= 255)): bad.append("0 <= lo <= hi <= 255")
    if not np.all((v["lo"] + v["ef"] >= 0) & (v["hi"] + v["ef"] <= 255)): bad.append("lo + ef >= 0 and hi + ef <= 255")
    for k in ("s0", "dr"):
        if not np.all((v[k] >= 0) & (v[k] <= 255)): bad.append("range of " + k)
    if not np.all((d["wt"] >= 0) & (d["wt"] <= 2047)): bad.append("range of wt")
    return bad
def reference(lo, hi, ef, s0, wt, dr):
    tl, th, te, s, d = [x.astype(np.float32).astype(np.int64).reshape(N, 8, 16, -1) for x in (lo, hi, ef, s0, dr)]
    w = wt.astype(np.int64).reshape(N, 8, 16, 2); st = [s[r] for r in range(N)]; y = np.zeros((N, 8, ST, L), np.int64); old = []
    for t in range(ST):
        now = []
        for r in range(N):
            x = st[r]; c = probes(x, w[r]); ix = c.reshape(8, 1, P * L)
            a = np.take_along_axis(tl[r], ix, 2).reshape(8, 16, P, L); b = np.take_along_axis(th[r], ix, 2).reshape(8, 16, P, L)
            ok = np.all((a <= x[:, :, None, :]) & (x[:, :, None, :] <= b), axis=1)
            fired = np.any(ok, axis=1); i = np.argmax(ok, axis=1)
            col = np.take_along_axis(c, i[:, None, :], 1); place = np.take_along_axis(c, np.maximum(i - 1, 0)[:, None, :], 1)[:, 0]
            fl, fh, fe = [np.take_along_axis(v[r], col, 2) for v in (tl, th, te)]
            y[r, :, t] = np.where(fired, i, P)
            st[r] = np.where(fired[:, None, :], x + fe, np.abs(x - d[r, :, :, t:t + 1]))
            now.append((fired, fl, fh, fe, place))
        if t > 0:
            for r in range(N):
                f0, l0, h0, e0, p0 = old[r]; f1, l1, h1, e1, p1 = now[(r + 1) % N]
                cl = np.maximum(l0, l1 - e0); ch = np.minimum(h0, h1 - e0); ce = e0 + e1
                for g in range(8):
                    m = np.flatnonzero(f0[g] & f1[g]); cols, first = np.unique(p0[g][m], return_index=True); k = m[first]
                    tl[r, g][:, cols] = cl[g][:, k]; th[r, g][:, cols] = ch[g][:, k]; te[r, g][:, cols] = ce[g][:, k]
        old = now
        if t < ST - 1: st = [st[(r - 1) % N] for r in range(N)]
    return {"ys": np.stack(st).reshape(N, 128, L).astype(np.float32), "yp": y.reshape(N, 8, ST * L).astype(np.float32)}

from concourse.bass import DstId, RemoteDMATransfer
from concourse.mybir import AluOpType as A, ActivationFunctionType as F

W, OFF, ST, H, REP = 4096, 32, 4, 128, 3
WW = W + OFF
BIG, SH = 1.5 * 2.0 ** 23 * W, W // 2 - 0.5 + OFF
SG = SH - 16384
NV = [(12, 10), (11, 7), (9, 11), (6, 15), (5, 10), (11, 9), (9, 8), (6, 11)]
PR = [1000.0, 2000.0, 2000.0, 1000.0, 1000.0, 0.0, 0.0]

SCRATCH = {}
for _x in range(2):
    for _n, _c, _d in (("tv", 4096, "bfloat16"), ("raw", 4096, "bfloat16"), ("yt", H, "float32"), ("yi", H, "float32"),
                       ("ps", H, "float32"), ("ix", H, "uint16"), ("va", H, "float32"), ("fa", H, "float32"),
                       ("vb", H, "float32"), ("fb", H, "float32"), ("fu", 8, "uint16"), ("nd", H, "bfloat16"),
                       ("t1", H, "bfloat16"), ("pb", H, "float32"), ("ee", H, "bfloat16"), ("wn", H, "bfloat16"),
                       ("wa", 8, "float32"), ("of", 16, "uint16"), ("rq", 2 * H, "bfloat16")):
        SCRATCH["%s%d" % (_n, _x)] = ("sbuf", [128, _c], _d)
    SCRATCH["hh%d" % _x] = ("sbuf", [128, 4, 32], "bfloat16")
    SCRATCH["nn%d" % _x] = ("sbuf", [128, 4, 32], "bfloat16")
for _n, _c, _d in (("lot", WW, "bfloat16"), ("hit", WW, "bfloat16"), ("eft", WW, "bfloat16"), ("iot", WW, "float32"),
                   ("sr", 8 * REP * H, "bfloat16"), ("pp", 2 * H, "float32"), ("idf", H, "float32"), ("ch", H, "bfloat16"),
                   ("pu", 32, "uint16"), ("pw", 32, "float32"), ("ngs", 4 * H, "bfloat16"), ("nge", 4 * H, "bfloat16"),
                   ("flo", 4 * H, "bfloat16"), ("fli", 4 * H, "bfloat16"), ("lbo", 8 * H, "bfloat16"), ("lbi", 8 * H, "bfloat16"),
                   ("qo", 8 * H, "bfloat16"), ("qi", 8 * H, "bfloat16"), ("sno", 6 * H, "bfloat16"), ("sbi", 4 * H, "bfloat16"),
                   ("yps", 256, "float32"), ("yss", 256, "float32"),
                   ("wti", 2, "int32"), ("wtf", 2, "float32"), ("drb", 4, "bfloat16"), ("ngd", 4, "float32"),
                   ("r8", 8, "float32"), ("rk", H, "float32"), ("k2", 16, "float32"),
                   ("pi", 8, "int32"), ("pj", 8, "int32"), ("pf", 16, "float32"),
                   ("idn", H, "bfloat16"), ("nid", H, "bfloat16"), ("zs", 144, "bfloat16"), ("blk", H, "bfloat16"),
                   ("tri", H, "bfloat16"), ("tl", H, "bfloat16"), ("yy", H, "bfloat16"), ("zz", 640, "bfloat16"),
                   ("yn", H, "bfloat16"), ("k0", H, "bfloat16"), ("rp", H, "bfloat16"), ("d0", H, "float32"), ("dw", H, "bfloat16"),
                   ("ro", 8, "uint16"), ("ci", 8, "uint16"), ("kc", H, "bfloat16"), ("c1", 16, "int32"), ("c2", 32, "int32")):
    SCRATCH[_n] = ("sbuf", [128, _c], _d)
SCRATCH["sl"] = ("sbuf", [128, 32, 32], "bfloat16")
SCRATCH["c3"] = ("sbuf", [128, 4, 16], "bfloat16")
SCRATCH["cc"] = ("sbuf", [128, 4, 144], "bfloat16")
for _n in ("pc0", "pc1", "pd0", "pd1", "pt", "pm"):
    SCRATCH[_n] = ("psum", [128, 512], "float32")
for _n in ("py0", "py1"):
    SCRATCH[_n] = ("psum", [128, 16, 32], "float32")

SEMAPHORES = ["V", "S", "P", "G", "sent"] + ["d%d" % _i for _i in range(24)] + ["m%d" % _i for _i in range(24)]

CY, GA, SC, PE = 1.04, 1.56, 3.8, 0.5


def _masks(topo, c, nxt, prv):
    a, b = topo.engines(c, nxt), topo.engines(c, prv)
    if len(a) == len(b):
        a, b = a[:len(a) // 2], [e for e in b if e not in a[:len(a) // 2]]
    elif len(a) > len(b):
        a = [e for e in a if e not in b]
    else:
        b = [e for e in b if e not in a]
    out = []
    for es in (a, b):
        n = 1
        while 2 * n <= len(es):
            n *= 2
        out.append((sum(1 << e for e in es[:n]), n))
    return out


def rank_program(g, core, T, topo):
    rank = T.rank_of(core)
    if rank is None:
        return
    cores = list(T.cores)
    N = len(cores)
    nxt, prv = cores[(rank + 1) % N], cores[(rank - 1) % N]
    (mk_n, n_n), (mk_p, n_p) = _masks(topo, core, nxt, prv)
    in_p = _masks(topo, prv, core, cores[(rank - 2) % N])[0][1]
    in_n = _masks(topo, nxt, cores[(rank + 2) % N], core)[1][1]
    Q = {"V": g.vector, "S": g.scalar, "P": g.tensor, "G": g, "Y": g.sync}
    V, S, P = g.vector, g.scalar, g.tensor

    ops, lastw, readers = [], {}, {}
    pri = [0.0]
    cnt = {"d": 0, "m": 0, "sent": 0}

    def op(eng, fn, r, w, dur, lat=0.0, sem=None):
        deps = set()
        for x in r:
            if x in lastw:
                deps.add(lastw[x])
        for x in w:
            if x in lastw:
                deps.add(lastw[x])
            deps.update(readers.get(x, []))
        i = len(ops)
        for x in r:
            readers.setdefault(x, []).append(i)
        for x in w:
            lastw[x] = i
            readers[x] = []
        ops.append({"e": eng, "f": fn, "d": sorted(deps), "t": dur, "l": lat, "s": sem, "w": w, "p": pri[0]})
        return i

    def vop(fn, r, w, n, c=1.0):
        op("V", fn, r, w, 45 + max(64, n * c) * CY)

    def ts(out, in0, s1, s2, o0, o1, r, w, n, c=1.0):
        if o1 is None:
            vop(lambda: V.tensor_scalar(out, in0, s1, None, o0), r, w, n, c)
        else:
            vop(lambda: V.tensor_scalar(out, in0, s1, s2, o0, o1), r, w, n, c)

    def tt(out, in0, in1, o, r, w, n, c=2.0):
        vop(lambda: V.tensor_tensor(out, in0, in1, o), r, w, n, c)

    def cp(out, in_, r, w, n, c=1.0):
        vop(lambda: V.tensor_copy(out, in_), r, w, n, c)

    def act(out, in_, f, r, w, n, c=1.0, bias=0.0, scale=1.0):
        op("S", lambda: S.activation(out, in_, f, bias=bias, scale=scale), r, w, 65 + max(64, n * c) * CY)

    def mms(lst, r, w, new=True, done=True):
        def fn():
            last = None
            for k, (o, l, x, n) in enumerate(lst):
                last = P.matmul(o, l, x, new and k == 0, done and k == len(lst) - 1)
            return last
        op("P", fn, r, w, sum(max(64, m[3]) for m in lst) * PE, 60)

    def dma(eng, pairs, r, w, lat):
        sem = T.sem["d%d" % cnt["d"]]
        cnt["d"] += 1

        def fn():
            for out, in_ in pairs:
                Q[eng].dma_start(out, in_).then_inc(sem, 16)
        op(eng, fn, r, w, 60 * len(pairs), lat, (sem, 16 * len(pairs)))

    def send(parts, r):
        tr = []
        arr = []
        for src, dst, fwd, name in parts:
            sem = T.sem["m%d" % cnt["m"]]
            cnt["m"] += 1
            rid, pid, _ = topo.addr(nxt if fwd else prv)
            tr.append((src, dst, sem, rid, pid, mk_n if fwd else mk_p))
            cnt["sent"] += n_n if fwd else n_p
            arr.append((name, sem, in_p if fwd else in_n))

        def fn():
            if len(tr) == 1:
                src, dst, sem, rid, pid, m = tr[0]
                return g.remote_dma(dst, src, sem, T.sem.sent, pid, rid, m)
            return g.remote_dma_fused([RemoteDMATransfer(dst_ids=[DstId(rid=rid, pnc=pid)], dma_engine_mask=m, remote_sem=sem,
                                                         src=src, dst=dst) for src, dst, sem, rid, pid, m in tr], local_sem=T.sem.sent)
        i = op("G", fn, r, [], 600)
        for name, sem, n in arr:
            j = op("-", None, [], [name], 0, 3000, (sem, n))
            ops[j]["d"] = [i]

    def halves(out, lh, rhs, b0):
        return [(out[:, 0:4, 16 * h:16 * h + 16], l, rhs[:, b0:b0 + 4, 16 * e:16 * e + 16], 64)
                for h in range(2) for e in range(2) for l in lh(h, e)]

    sl = lambda j: T.sl[:, 4 * j:4 * j + 4, :]
    sr = lambda j, a, b: T.sr[:, (REP * j + a) * H:(REP * j + b) * H]

    tabs = {"lo": T.lot, "hi": T.hit, "ef": T.eft}
    dma("Y", [(T.wti[:], T.wt[:])], [], ["wti"], 2200)
    dma("Y", [(T.lot[:, OFF:WW], T.lo[:])], [], ["lo"], 6000)
    dma("Y", [(T.hit[:, OFF:WW], T.hi[:])], [], ["hi"], 9500)
    dma("Y", [(T.eft[:, OFF:WW], T.ef[:])], [], ["ef"], 13000)
    for x in range(2):
        src = T.s0[:, (1 - x) * H:(2 - x) * H]
        dma("S", [(sl(x), src)], [], ["sl%d" % x], 2300)
        dma("S", [(sr(x, k, k + 1), src) for k in range(REP)], [], ["sr%d" % x], 2500)
    dma("S", [(T.drb[:], T.dr[:])], [], ["drb"], 2600)
    for i, o in enumerate(ops):
        o["p"] = 1e6 - 1e5 * i

    def iota(out, pat, base, cm, w, n, flag=True):
        if flag:
            op("G", lambda: g.iota(out, pat, base, cm, allow_small_or_imprecise_dtypes=True), [], [w], 130 + 2 * n * CY)
        else:
            op("G", lambda: g.iota(out, pat, base, cm), [], [w], 130 + 2 * n * CY)

    def sel(out, in_, pat, cmp_, fill, base, cm, r, w):
        op("G", lambda: g.affine_select(out, in_, pat, cmp_, fill, base, cm), r, w, 170 + 2 * H * CY)
    iota(T.pi[:, 0:1], [[0, 1]], 0, 1, "pi", 1, False)
    iota(T.k2[:], [[2, 16]], 0, 0, "k2", 16)
    iota(T.rk[:], [[0, 8], [1, 16]], 0, 0, "rk", H)
    iota(T.r8[:], [[1, 8]], 0, 0, "r8", 8)
    for k in range(8):
        iota(T.iot[:, 516 * k:516 * k + 516], [[1, 516]], 516 * k, 0, "iot%d" % k, 516)
    for n, v in (("idn", 1.0), ("nid", -1.0)):
        vop(lambda n=n, v=v: V.memset(T[n][:], v), [], [n], 64)
        sel(T[n][:], T[n][:], [[-1, H]], A.is_equal, 0.0, 0, 1, [], [n])
    vop(lambda: V.memset(T.blk[:], -256.0), [], ["blk"], 64)
    sel(T.blk[:], T.blk[:], [[-16, 8], [0, 16]], A.is_ge, 0.0, 0, 1, [], ["blk"])
    sel(T.blk[:], T.blk[:], [[16, 8], [0, 16]], A.is_ge, 0.0, 15, -1, [], ["blk"])
    iota(T.zs[:, H:144], [[0, 16]], 0, 0, "zsb", 16)
    sel(T.zs[:, 0:H], T.blk[:], [[0, 8], [1, 16]], A.is_equal, 0.0, -15, 0, ["blk"], ["zs"])
    sel(T.tri[:], T.blk[:], [[1, H]], A.is_ge, 0.0, 0, -1, ["blk"], ["tri"])
    sel(T.tl[:], T.blk[:], [[-1, H]], A.is_gt, 0.0, 0, 1, ["blk"], ["tl"])
    sel(T.yy[:], T.tri[:], [[1, H]], A.not_equal, 256.0, 0, -1, ["tri"], ["yy"])
    vop(lambda: V.memset(T.zz[:], 0.0), [], ["zz0", "zz1", "zz2", "zz3"], 320)
    for h in range(2):
        sel(T.zz[:, 160 * h + 16:160 * h + 144], T.yy[:], [[0, 4], [1, 2], [0, 16]], A.is_equal, 0.0, -h, 0, ["yy"], ["zz%d" % h])
    act(T.yn[:], T.idn[:], F.Identity, ["idn"], ["yn"], H, scale=256.0)
    sel(T.yn[:], T.yn[:], [[0, 8], [1, 16]], A.not_equal, 0.0, 0, 0, [], ["yn"])
    sel(T.yn[:], T.yn[:], [[-1, H]], A.not_equal, -256.0, -1, 1, [], ["yn"])
    sel(T.yn[:], T.yn[:], [[0, 8], [1, 16]], A.not_equal, 0.0, -15, 0, [], ["yn"])
    for h in range(2):
        sel(T.zz[:, 320 + 160 * h + 16:320 + 160 * h + 144], T.yn[:], [[0, 4], [1, 2], [0, 16]], A.is_equal, 0.0, -h, 0, ["yn"], ["zz%d" % (2 + h)])
    iota(T.d0[:], [[0, H]], 0, 0, "d0", H)
    sel(T.d0[:], T.d0[:], [[0, 8], [1, 16]], A.not_equal, -1048576.0, 0, 0, [], ["d0"])
    for n in ("lo", "hi", "ef"):
        iota(tabs[n][:, 0:OFF], [[0, OFF]], -512 if n == "ef" else 0, 0, n + "h", OFF)
    vop(lambda: V.memset(T.cc[:], 0.0), [], ["cc%d" % k for k in range(4)], 288)
    pi0 = T.pi[:, 0:1]
    ts(T.pj[:, 0:1], pi0, 15, None, A.bitwise_and, None, ["pi"], ["pj0"], 1)
    ts(T.pj[:, 1:2], pi0, 4, 1, A.logical_shift_right, A.bitwise_and, ["pi"], ["pj1"], 1)
    ts(T.pj[:, 2:3], pi0, 7, None, A.bitwise_and, None, ["pi"], ["pj2"], 1)
    ts(T.pj[:, 3:4], pi0, 3, 1, A.logical_shift_right, A.bitwise_and, ["pi"], ["pj3"], 1)
    cp(T.pf[:, 0:4], T.pj[:, 0:4], ["pj%d" % k for k in range(4)], ["pf"], 4)
    col = lambda k: T.pf[:, k:k + 1]
    ic = col(0)
    ts(col(4), col(1), -1.0, 1.0, A.mult, A.add, ["pf"], ["pf4"], 1)
    ts(col(5), col(2), 16.0, col(3), A.mult, A.add, ["pf"], ["pf5"], 1)
    ts(col(6), ic, 16.0, None, A.add, None, ["pf"], ["pf6"], 1)
    ts(T.ro[:], T.r8[:], 2.0, col(5), A.mult, A.add, ["r8", "pf5"], ["ro"], 8)
    cp(T.ci[:], T.r8[:], ["r8"], ["ci"], 8)
    ts(T.rp[:], T.rk[:], ic, -2048.0, A.is_equal, A.mult, ["rk", "pf"], ["rp"], H)
    act(T.dw[:], T.rp[:], F.Identity, ["rp"], ["dw"], H, bias=1.0, scale=1.0 / 1024)
    sel(T.dw[:], T.dw[:], [[0, 8], [1, 16]], A.not_equal, 0.0, 0, 0, [], ["dw"])
    ts(col(7), ic, 0.5, None, A.add, None, ["pf"], ["pf7"], 1)
    act(T.kc[:], T.rk[:], F.Identity, ["rk", "pf7"], ["kc"], H, bias=col(7), scale=0.0)
    act(T.k0[:], T.kc[:], F.Relu, ["kc"], ["k0"], H, bias=32768.0, scale=-32768.0)
    iota(T.ch[:], [[0, H]], W // 2, 0, "ch", H)
    act(T.idf[:], T.idn[:], F.Copy, ["idn"], ["idf"], H)
    act(T.ngd[:], T.drb[:], F.Identity, ["drb"], ["ngd"], 4, scale=-1.0)
    cp(T.wtf[:, 1:2], T.wti[:, 1:2], ["wti"], ["wtf"], 2)
    ts(T.wtf[:, 0:1], T.wti[:, 0:1], W // 2.0, None, A.add, None, ["wti"], ["wtg"], 2)
    ts(T.c1[:], T.k2[:], T.wtf[:, 1:2], T.wtf[:, 0:1], A.mult, A.add, ["k2", "wtf", "wtg"], ["c1"], 16)
    ts(T.c2[:, 0:16], T.c1[:], W - 64, None, A.bitwise_and, None, ["c1"], ["c20"], 16)
    ts(T.c2[:, 16:32], T.c1[:], 63, None, A.bitwise_and, None, ["c1"], ["c21"], 16)
    for h in range(2):
        for q in range(2):
            ts(T.c3[:, 2 * h + q, :], T.c2[:, 16 * q:16 * q + 16], 0.0 if q else -W // 2.0, col(1) if h else col(4), A.add, A.mult,
               ["c2%d" % q, "pf", "pf4"], ["c3%d%d" % (h, q)], 16)
    for a in range(4):
        o, i = T.cc[32 * a:32 * a + 32, :, 16 + 32 * a:32 + 32 * a], T.c3[32 * a:32 * a + 32, :, :]
        if a % 2:
            act(o, i, F.Copy, ["c300", "c301", "c310", "c311"], ["cc%d" % a], 64)
        else:
            cp(o, i, ["c300", "c301", "c310", "c311"], ["cc%d" % a], 64)

    acc = {}
    dbank = [0]

    def index(t, x):
        j, X = 2 * t + x, str(x)
        sn = "sl%d" % j
        py, pn, p0, ps = T["py" + X], "pp" + X, x * H, T["ps" + X]
        if t > 0:
            dma("Y", [(sr(j, k, k + 1), sl(j)) for k in range(REP)], [sn], ["sr%d" % j], 2200)
        lh = lambda h, e: [T.cc[:, 2 * h + q, 16 * (1 - e):16 * (1 - e) + H] for q in range(2)]
        mms([(py[:, 0:4, :], T.idn[:], T.kc[:], H), (py[:, 0:4, :], T.idn[:], T.ch[:], H)] + halves(py, lh, T.sl, 4 * j),
            [sn, "cc0", "cc1", "cc2", "cc3", "idn", "kc", "ch"], ["py" + X])
        act(T["yt" + X][:], py[:, 0:4, :], F.Identity, [], ["py" + X, "yt" + X], H, bias=BIG)
        act(T["yi" + X][:], T["yt" + X][:], F.Identity, ["yt" + X], ["yi" + X], H, bias=BIG, scale=-1.0)
        tt(ps[:], T["yi" + X][:], py[:, 0:4, :], A.add, ["yi" + X], ["py" + X, "ps" + X], H, 1.0)
        vop(lambda: V.transpose(T.pp[:, p0:p0 + H], ps[:]), ["ps" + X], [pn], H)
        ts(T["ix" + X][:], T.pp[:, p0:p0 + H].indirect(T.ro[:, 0:8]), SH, None, A.add, None, [pn, "ro"], ["ix" + X], H, GA)
        mms([(py[:, 0:4, :], T.idf[:], ps[:], 4 * H)], ["ps" + X, "idf"], ["py" + X], True, False)
        act(T["nd" + X][:], sl(j), F.Abs, [sn, "ngd"], ["nd" + X], H, bias=T.ngd[:, t:t + 1])
        if t < 2:
            act(T.ngs[:, j * H:(j + 1) * H], sl(j), F.Identity, [sn], ["ngs%d" % j], H, scale=-1.0)

    def count(t, x, u0, k0, n, name):
        X = str(x)

        def fn():
            last = None
            for k in range(n):
                acc[(t, x)] = acc.get((t, x), 0) + 1
                last = P.matmul(T["pc" + X][:, 0:H], T.zs[:, 15 - k0 - k:15 - k0 - k + H], T["tv" + X][:, (u0 + k) * H:(u0 + k + 1) * H],
                                acc[(t, x)] == 1, acc[(t, x)] == 32)
            return last
        op("P", fn, [name, "zs", "zsb", "pc" + X], [], n * H * PE, 60)

    def test(t, x, b, k0, n, eng):
        X, j = str(x), 2 * t + x
        u0 = k0 + (16 if b == "hi" else 0)
        names = ["tv%d_%d" % (x, u0 + k) for k in range(n)]
        win = tabs[b][:, 0:WW].indirect(T["ix" + X][:, 8 * k0:8 * (k0 + n)])
        out = T["tv" + X][:, u0 * H:(u0 + n) * H]
        if eng == "V":
            tt(out, win, sr(j, 0, n), A.is_gt if b == "lo" else A.is_lt, [b, b + "h", "ix" + X, "sr%d" % j], names, n * H, GA)
        else:
            raw = T["raw" + X][:, u0 * H:(u0 + n) * H]
            pd = "pd%d" % dbank[0]
            dbank[0] ^= 1
            act(raw, win, F.Copy, [b, b + "h", "ix" + X], ["r" + k for k in names], n * H, GA)
            mms([(T[pd][:, 0:n * H], T.idn[:], raw, n * H)] + [(T[pd][:, k * H:(k + 1) * H], T.nid[:], sl(j), H) for k in range(n)],
                ["r" + k for k in names] + ["idn", "nid", "sl%d" % j], [pd])
            act(out, T[pd][:, 0:n * H], F.Relu, [], [pd] + names, n * H, scale=1.0 if b == "lo" else -1.0)
        i = len(ops)
        count(t, x, u0, k0, n, names[0])
        for k in names[1:]:
            readers[k].append(i)

    def groups(a, b, m):
        k = -(-(b - a) // m)
        cuts = [a + (b - a) * j // k for j in range(k + 1)]
        return [(cuts[j], cuts[j + 1] - cuts[j]) for j in range(k)]

    def tests(t, x, b, which=None):
        nv = NV[2 * t + x][b == "hi"]
        for k0, n in groups(0, nv, REP):
            if which in (None, 0):
                test(t, x, b, k0, n, "V")
        for j, (k0, n) in enumerate(groups(nv, 16, 4)):
            if which is None or (which == 0) == (j == 0):
                test(t, x, b, k0, n, "S")

    def post(t, x):
        X, hh = str(x), T["hh%d" % x]
        py = T["py" + X]
        j, jb = 2 * t + x, 2 * (t - 1) + x
        act(hh[:], T["pc" + X][:, 0:H], F.Relu, [], ["pc" + X, "hh" + X], H, bias=64.0, scale=0.25)
        lz = lambda m: lambda h, e: [T.zz[:, 320 * m + 176 * h + 16 - 16 * e:320 * m + 176 * h + 16 - 16 * e + H]]
        mms(halves(py, lz(0), hh, 0), ["hh" + X, "zz0", "zz1"], ["py" + X], False)
        if t in (1, 2):
            mms([(T.pm[:, 0:H], T.tl[:], T.rp[:], H), (T.pm[:, 0:H], T.blk[:], hh[:], H)], ["hh" + X, "tl", "rp", "blk"], ["pm"])
            act(T.flo[:, jb * H:(jb + 1) * H], T.pm[:, 0:H], F.Identity, [], ["pm", "flo%d" % jb], H, scale=-0.5)
            send([(T.flo[:, jb * H:(jb + 1) * H], T.fli[:, jb * H:(jb + 1) * H], False, "fli%d" % jb)], ["flo%d" % jb])
        mms([(T.pt[:, 0:H], T.idn[:], T["nd" + X][:], H), (T.pt[:, 0:H], T.blk[:], hh[:], H)], ["hh" + X, "idn", "nd" + X, "blk"], ["pt"])
        va, fa, fu = T["va" + X], T["fa" + X], T["fu" + X]
        vop(lambda: V.transpose(va[:], py[:, 0:4, :]), [], ["py" + X, "va" + X], H)
        vop(lambda: V.tensor_tensor_scan(fa[:], T.d0[:], va[:], 0.0, A.add, A.max), ["d0", "va" + X], ["fa" + X], H)
        ts(fu[:], fa[:, 15:H:16], SG, None, A.add, None, ["fa" + X], ["fu" + X], 8)
        fired = lambda b: tabs[b][:, 0:WW].indirect(fu[:, 0:8])
        if t in (1, 2):
            for q, (b, o) in enumerate((("lo", A.max), ("hi", A.min))):
                a = (2 * jb + q) * H
                tt(T.lbo[:, a:a + H], fired(b), T.qi[:, a:a + H], o, [b, b + "h", "fu" + X, "qi%d" % jb], ["lbo%d%d" % (jb, q)], H, GA)
            a = 2 * jb * H
            send([(T.lbo[:, a:a + 2 * H], T.lbi[:, a:a + 2 * H], False, "lbi%d" % jb)], ["lbo%d0" % jb, "lbo%d1" % jb])
        tt(T["t1" + X][:], fired("ef"), sr(j, 0, 1), A.add, ["ef", "efh", "fu" + X, "sr%d" % j], ["t1" + X], H, GA)
        if t < ST - 1:
            so = T.sno[:, j * H:(j + 1) * H]
            tt(so, T["t1" + X][:], T.pt[:, 0:H], A.max, ["t1" + X], ["pt", "sno%d" % j], H, 1.0)
            parts = [(so, sl(j + 2), True, "sl%d" % (j + 2))]
            if t > 0:
                parts.append((so, T.sbi[:, jb * H:(jb + 1) * H], False, "sbi%d" % jb))
            send(parts, ["sno%d" % j])
        else:
            a = (1 - x) * H
            tt(T.yss[:, a:a + H], T["t1" + X][:], T.pt[:, 0:H], A.max, ["t1" + X], ["pt", "yss" + X], H, 1.0)
            dma("Y", [(T.ys[:, a:a + H], T.yss[:, a:a + H])], ["yss" + X], ["ys" + X], 2000)
        if t < 2:
            ne = T.nge[:, j * H:(j + 1) * H]
            act(ne, fired("ef"), F.Identity, ["ef", "efh", "fu" + X], ["nge%d" % j], H, GA, scale=-1.0)
            rq = T["rq" + X]
            for q, b in enumerate(("lo", "hi")):
                act(rq[:, q * H:(q + 1) * H], fired(b), F.Copy, [b, b + "h", "fu" + X], ["rq%d%d" % (x, q)], H, GA)
            mms([(T.pt[:, H:3 * H], T.idn[:], rq[:], 2 * H)] + [(T.pt[:, (1 + q) * H:(2 + q) * H], T.nid[:], ne, H) for q in range(2)],
                ["rq%d0" % x, "rq%d1" % x, "nge%d" % j, "idn", "nid"], ["pt"])
            a = 2 * j * H
            act(T.qo[:, a:a + 2 * H], T.pt[:, H:3 * H], F.Copy, [], ["pt", "qo%d" % j], 2 * H)
            send([(T.qo[:, a:a + 2 * H], T.qi[:, a:a + 2 * H], True, "qi%d" % j)], ["qo%d" % j])
        mms([(T.pm[:, H:2 * H], T.tri[:], hh[:], H)], ["hh" + X, "tri"], ["pm"])
        nn = T["nn" + X]
        act(nn[:], T.pm[:, H:2 * H], F.Relu, [], ["pm", "nn" + X], H, bias=64.0)
        if t < 2:
            vb, fb = T["vb" + X], T["fb" + X]
            mms([(py[:, 0:4, :], T.idf[:], T["ps" + X][:], 4 * H), (py[:, 0:4, :], T.idn[:], T.k0[:], H)] + halves(py, lz(1), nn, 0),
                ["ps" + X, "nn" + X, "zz2", "zz3", "idn", "idf", "k0"], ["py" + X])
            vop(lambda: V.transpose(vb[:], py[:, 0:4, :]), [], ["py" + X, "vb" + X], H)
            vop(lambda: V.tensor_tensor_scan(fb[:], T.d0[:], vb[:], 0.0, A.add, A.max), ["d0", "vb" + X], ["fb" + X], H)
            ts(T.pu[:, 8 * j:8 * j + 8], fb[:, 15:H:16], SG, None, A.add, None, ["fb" + X], ["pu%d" % j], 8)
            ts(T.pw[:, 8 * j:8 * j + 8], fb[:, 15:H:16], SG, 0.0, A.add, A.max, ["fb" + X], ["pw%d" % j], 8)
        mms([(T.pm[32 * t:32 * t + 32, (3 - x) * H:(4 - x) * H], T.blk[:, 0:H:4], nn[:], H)], ["nn" + X, "blk"], ["pm"])

    def choose(t, x):
        X, j = str(x), 2 * (t - 1) + x
        pw = T.pw[:, 8 * j:8 * j + 8]
        tt(T["pb" + X][:], T.iot[:, 0:WW].indirect(T.pu[:, 8 * j:8 * j + 8]), T.fli[:, j * H:(j + 1) * H], A.min,
           ["iot%d" % k for k in range(8)] + ["pu%d" % j, "fli%d" % j], ["pb" + X], H, GA)
        tt(T["ee" + X][:], pw.indirect(T.ci[:, 0:8]), T["pb" + X][:], A.is_equal, ["pw%d" % j, "ci", "pb" + X], ["ee" + X], H, GA)
        vop(lambda: V.tensor_tensor_scan(T["wn" + X][:], T.dw[:], T["ee" + X][:], 0.0, A.mult, A.add), ["dw", "ee" + X], ["wn" + X], H, 0.5)
        tt(T["wa" + X][:], T["wn" + X][:, 15:H:16], pw, A.mult, ["wn" + X, "pw%d" % j], ["wa" + X], 8)
        ts(T["of" + X][:, 0:16:2], T["wa" + X][:], col(6), None, A.max, None, ["wa" + X, "pf6"], ["of" + X], 8)

    def update(t, x, which):
        X, j = str(x), 2 * (t - 1) + x
        for c in range(7, -1, -1):
            for b in which:
                if b == "ef":
                    i0, i1, r = T.sbi[:, j * H + 16 * c:j * H + 16 * c + 16], T.ngs, ["sbi%d" % j, "ngs%d" % j]
                else:
                    a = (2 * j + (b == "hi")) * H + 16 * c
                    i0, i1, r = T.lbi[:, a:a + 16], T.nge, ["lbi%d" % j, "nge%d" % j]
                tt(tabs[b][:, 0:WW].indirect(T["of" + X][:, 2 * c:2 * c + 1]), i0, i1[:, j * H + 16 * c:j * H + 16 * c + 16], A.add,
                   r + ["of" + X], [b, b + "h"], 16, SC)

    def numbers(t0, t1, eng):
        a, b = 32 * t0, 32 * t1
        act(T.yps[a:b, :], T.pm[a:b, 2 * H:4 * H], F.Identity, [], ["pm", "yp%d" % t0], 2 * H, scale=-1.0 / 16384)
        dma(eng, [(T.yp[:, 256 * t:256 * t + 256], T.yps[32 * t:32 * t + 32:4, :]) for t in range(t0, t1)], ["yp%d" % t0], ["yq%d" % t0], 2000)

    def do(p, f, *a):
        pri[0] = PR[p]
        f(*a)
        pri[0] = 0.0

    for t in range(ST):
        do(0, index, t, 0)
        do(1, index, t, 1)
        if t == 0:
            do(2, tests, t, 0, "lo")
            tests(t, 1, "lo", 0)
            do(2, tests, t, 0, "hi")
            do(3, post, t, 0)
            tests(t, 1, "lo", 1)
            tests(t, 1, "hi")
        else:
            do(2, tests, t, 0, "hi")
            do(2, tests, t, 0, "lo")
            do(3, post, t, 0)
            tests(t, 1, "hi")
            tests(t, 1, "lo")
        do(4, post, t, 1)
        if t in (1, 2):
            for x in range(2):
                do(5 + x, choose, t, x)
                update(t, x, ("hi", "lo"))
                update(t, x, ("ef",))
        if t == 2:
            numbers(0, 3, "Y")
    numbers(3, 4, "S")

    n = len(ops)
    succ = [[] for _ in range(n)]
    for i, o in enumerate(ops):
        for d in o["d"]:
            succ[d].append(i)

    def gap(d, i):
        a, b = ops[d]["e"], ops[i]["e"]
        return ops[d]["l"] + (0 if a == b == "P" else 60 if a == b else 100)
    up = [0.0] * n
    for i in range(n - 1, -1, -1):
        up[i] = ops[i]["t"] + max([gap(i, k) + up[k] for k in succ[i]] + [ops[i]["l"]])
    left = [len(o["d"]) for o in ops]
    ready = [0.0] * n
    pool = [i for i in range(n) if left[i] == 0]
    free = {e: 0.0 for e in "VSPGY-"}
    order = {e: [] for e in "VSPGY-"}
    while pool:
        at = lambda k: max(ready[k], free[ops[k]["e"]])
        i0 = min(pool, key=at)
        e, first = ops[i0]["e"], at(i0)
        i = max([k for k in pool if ops[k]["e"] == e and ready[k] <= first + 80], key=lambda k: (up[k] + ops[k]["p"], -k))
        pool.remove(i)
        st = at(i)
        ops[i]["at"] = st
        if e != "-":
            free[e] = st + ops[i]["t"]
        order[e].append(i)
        for k in succ[i]:
            ready[k] = max(ready[k], st + ops[i]["t"] + gap(i, k))
            left[k] -= 1
            if left[k] == 0:
                pool.append(k)

    for e in "VSPG":
        c = 0
        for i in order[e]:
            if ops[i]["s"] is None and any(ops[k]["e"] != "-" and not (e == "P" == ops[k]["e"]) for k in succ[i]):
                c += 1
                ops[i]["c"] = c
    for e in "VSPGY":
        seen = {}
        for i in order[e]:
            need = {}
            for d in ops[i]["d"]:
                o = ops[d]
                if o["s"] is not None:
                    need[("x", d)] = o["s"]
                elif not (e == "P" == o["e"]):
                    k = ("e", o["e"])
                    if k not in need or need[k][1] < o["c"]:
                        need[k] = (T.sem[o["e"]], o["c"])
            for k, (sem, c) in need.items():
                if seen.get(k, 0) < c:
                    seen[k] = c
                    Q[e].wait_ge(sem, c)
            ins = ops[i]["f"]()
            if "c" in ops[i]:
                ins.then_inc(T.sem[e], 1)
    for i in range(n):
        if ops[i]["s"] is not None and not succ[i]:
            g.wait_ge(ops[i]["s"][0], ops[i]["s"][1])
    g.wait_ge(T.sem.sent, cnt["sent"])
    return ops
